import numpy as np
import ml_dtypes


def mxq(x, axis, fmt="e4m3"):
    dtype, down = {"e4m3": (ml_dtypes.float8_e4m3fn, 7), "e5m2": (ml_dtypes.float8_e5m2, 14)}[fmt]
    v = np.moveaxis(np.asarray(x, np.float32).astype(ml_dtypes.bfloat16).astype(np.float64), axis, -1)
    blocks = v.reshape(v.shape[:-1] + (-1, 32))
    amax = np.abs(blocks).max(-1, keepdims=True)
    byte = np.maximum(np.where(amax > 0, np.frexp(amax)[1] - 1 + 127, 0) - down, 1)
    scale = np.exp2(byte - 127.0)
    codes = (blocks / scale).astype(np.float32).astype(dtype).astype(np.float64)
    return np.moveaxis((codes * scale).reshape(v.shape), -1, axis)


WIDE = False


def mx_kscale(k):
    if not WIDE:
        return np.ones(k)
    levels = np.array([10, -10, 5, -5, 0])
    if k % 512:
        return np.exp2(np.random.permutation(np.resize(levels, k // 32))).repeat(32)
    a = np.empty((k // 512, 16))
    for p in range(k // 512):
        a[p, :8] = np.random.permutation(np.resize(levels, 8))
        for g in range(8):
            far = levels[np.abs(levels - a[p, g]) >= 10]
            a[p, g + 8] = far[np.random.randint(len(far))]
    return np.exp2(a.ravel()).repeat(32)


def f64(x):
    return np.asarray(x).astype(np.float64)


def striped(idx):
    return np.tile(np.asarray(idx).reshape(-1, 16).T, (8, 1)).astype(np.uint16)


def unstriped(offs):
    return offs[:16].T.reshape(-1).astype(np.int64)


E2M1 = np.array([0.0, 0.5, 1.0, 1.5, 2.0, 3.0, 4.0, 6.0, -0.0, -0.5, -1.0, -1.5, -2.0, -3.0, -4.0, -6.0])


def pack_weight(w, fmt):
    k, n = w.shape
    w = f64(np.asarray(w, np.float32).astype(ml_dtypes.bfloat16)).reshape(k // 32, 32, n)
    amax = np.abs(w).max(1)
    if fmt == "e4m3":
        byte = np.frexp(amax)[1] - 1 + 127 - 7
    else:
        mant, ex = np.frexp(amax / 6.0)
        byte = np.where(mant > 0.5, ex, ex - 1) + 127
    byte = np.clip(np.where(amax > 0, byte, 1), 1, 254)
    scaled = (w * np.exp2(127.0 - byte)[:, None, :]).reshape(k, n).astype(np.float32)
    by_word = np.ascontiguousarray(scaled.reshape(k // 512, 128, 4, n).transpose(0, 1, 3, 2))
    if fmt == "e4m3":
        words = by_word.astype(ml_dtypes.float8_e4m3fn).view(np.uint8)
    else:
        c = by_word.astype(ml_dtypes.float4_e2m1fn).view(np.uint8) & 0xF
        words = (c[..., 0::2] | (c[..., 1::2] << 4)).reshape(k // 512, 128, 2 * n)
    return np.ascontiguousarray(words), np.ascontiguousarray(byte.astype(np.uint8).reshape(k // 512, 16, n))


def unpack_weight(words, scales, fmt):
    g, _, n = scales.shape
    words = np.ascontiguousarray(words).reshape(g, 128, n, -1)
    if fmt == "e4m3":
        vals = words.view(ml_dtypes.float8_e4m3fn).astype(np.float64)
    else:
        nib = np.empty((g, 128, n, 4), np.uint8)
        nib[..., 0::2] = words & 0xF
        nib[..., 1::2] = words >> 4
        vals = E2M1[nib]
    vals = vals * np.repeat(np.exp2(scales.astype(np.float64) - 127.0), 8, axis=1)[..., None]
    return vals.transpose(0, 1, 3, 2).reshape(g * 512, n)


D, T, I, J, U, Z, E, M = 512, 2048, 512, 512, 1024, 1024, 512, 1024


def setup_inputs():
    n = np.random.standard_normal
    idx = np.random.permutation(T)[:I]
    idx2 = np.random.permutation(U)[:J]
    idx3 = np.random.permutation(Z)[:J]
    idx4 = np.random.permutation(M)[:J]
    fd = mx_kscale(D)
    fi = mx_kscale(I)
    ti = np.ones(T)
    ti[idx] = fi
    keysp = pack_weight(n((D, T)) / fd[:, None], "e4m3")
    return {
        "keys_words": keysp[0],
        "keys_scales": keysp[1],
        "notes": (n((D, U)) * 1.0 / np.sqrt(D) * fd[:, None]).astype(np.float32),
        "users2": (n((D, Z)) * 1.0 / np.sqrt(D) * fd[:, None]).astype(np.float32),
        "rowf": (np.random.uniform(0.02, 0.08, (I, 1)) * fi[:, None]).astype(np.float32),
        "vals": (n((E, T)) / ti).astype(np.float32),
        "old": (1.0 * n((E, M))).astype(np.float32),
        "offs": striped(idx),
        "offs2": striped(idx2),
        "offs3": striped(idx3),
        "offs4": striped(idx4),
    }


def reference(keys_words, keys_scales, notes, users2, rowf, vals, old, offs, offs2, offs3, offs4):
    idx = unstriped(offs)
    idx2 = unstriped(offs2)
    idx3 = unstriped(offs3)
    idx4 = unstriped(offs4)
    keysu = unpack_weight(keys_words, keys_scales, "e4m3")
    keysidxg = keysu[:, idx]
    notesq = mxq(f64(notes), 0, "e4m3")
    g1 = keysidxg.T @ notesq
    users2idx3q = mxq(f64(users2)[:, idx3], 0, "e4m3")
    g2 = keysidxg.T @ users2idx3q
    g0 = np.maximum(g1[:, idx2], g2)
    gr1 = g0 * f64(rowf)
    vt1 = f64(vals)[:, idx].T
    vt1q = mxq(vt1, 0, "e4m3")
    gr1q = mxq(gr1, 0, "e4m3")
    o = vt1q.T @ gr1q
    of = np.zeros((E, M))
    of[:, idx4] = o
    y = f64(old) + of
    return y

@@ -1,0 +1,216 @@
+from contextlib import ExitStack
+
+import concourse.mybir as mybir
+from concourse.masks import make_identity
+
+D, T, I, J, U, Z, E, M = 512, 2048, 512, 512, 1024, 1024, 512, 1024
+FLOPS = 2 * D * I * U + 2 * D * I * J + 2 * I * E * J
+
+F32 = mybir.dt.float32
+BF16 = mybir.dt.bfloat16
+I32 = mybir.dt.int32
+U32 = mybir.dt.uint32
+U16 = mybir.dt.uint16
+U8 = mybir.dt.uint8
+FP8X4 = mybir.dt.float8_e4m3fn_x4
+COPY = mybir.ActivationFunctionType.Copy
+ALU = mybir.AluOpType
+
+P = 128
+PACK = 4
+BANK = 512
+
+
+def tile_attend_tab_wideandown_put_kernel(
+    tc, keys_words, keys_scales, notes, users2, rowf, vals, old, offs, offs2, offs3, offs4, out
+):
+    nc = tc.nc
+    with ExitStack() as ctx:
+        sb = ctx.enter_context(tc.tile_pool(name="sb", bufs=1))
+        ring_a = ctx.enter_context(tc.psum_pool(name="ring_a", bufs=4))
+        ring_b = ctx.enter_context(tc.psum_pool(name="ring_b", bufs=4))
+
+        def tile(name, shape, dtype):
+            return sb.tile(shape, dtype, name=name, align_bytes=64)
+
+        def quantise(name, grouped, width, codes_name=None):
+            codes = tile(codes_name or name + "_codes", [P, width], U32)
+            scales = tile(name + "_scales", [P, width], U8)
+            nc.vector.quantize_mx(
+                out=codes[:].bitcast(FP8X4),
+                scales=scales[:],
+                in_=grouped[:].rearrange("p w t -> p (w t)"),
+            )
+            return codes, scales
+
+        def interleave(copy, grouped, planes):
+            copy(
+                grouped.rearrange("p (c i) t -> p c t i", i=4),
+                planes.rearrange("p t (c i) -> p c t i", i=4),
+            )
+
+        def product(bank, stationary, columns, moving):
+            nc.tensor.matmul_mx(
+                out=bank[:],
+                lhsT=stationary[0][:, columns].bitcast(FP8X4),
+                lhsT_scale=stationary[1][:, columns],
+                rhs=moving[0][:].bitcast(FP8X4),
+                rhs_scale=moving[1][:],
+                start=True,
+                stop=True,
+            )
+
+        token_list = tile("token_list", [P, I // 16], U16)
+        note_list = tile("note_list", [P, J // 16], U16)
+        user_list = tile("user_list", [P, J // 16], U16)
+        place_list = tile("place_list", [P, J // 16], U16)
+        key_words = tile("key_words", [P, T], U32)
+        key_bytes = tile("key_bytes", [P, T], U8)
+        notes_raw = [tile("notes_raw%d" % h, [P, PACK, BANK], F32) for h in range(U // BANK)]
+        users_raw = [tile("users_raw%d" % t, [P, Z], F32) for t in range(PACK)]
+        vals_raw = [tile("vals_raw%d" % b, [P, T], F32) for b in range(E // P)]
+        old_rows = [tile("old_rows%d" % b, [P, M], F32) for b in range(E // P)]
+        factors = tile("factors", [P, PACK], F32)
+
+        nc.gpsimd.memset(key_bytes[:].bitcast(I32), 0)
+        notes_by_place = notes.rearrange("(p t) u -> p t u", t=PACK)
+        users_by_place = users2.rearrange("(p t) z -> p t z", t=PACK)
+
+        nc.sync.dma_start(token_list[:], offs)
+        nc.sync.dma_start(user_list[:], offs3)
+        nc.sync.dma_start(note_list[:], offs2)
+        nc.sync.dma_start(out=factors[:], in_=rowf.rearrange("(p r) one -> p (r one)", r=PACK))
+        nc.sync.dma_start(out=notes_raw[0][:], in_=notes_by_place[:, :, 0:BANK])
+        for q in range(4):
+            nc.scalar.dma_start(
+                out=key_bytes[32 * q : 32 * q + 4, :].bitcast(I32),
+                in_=keys_scales[0, 4 * q : 4 * q + 4, :].bitcast(I32),
+            )
+        nc.sync.dma_start(
+            out=key_words[:].bitcast(I32),
+            in_=keys_words[0].rearrange("p n t -> p (n t)").bitcast(I32),
+        )
+        nc.sync.dma_start(out=notes_raw[1][:], in_=notes_by_place[:, :, BANK:U])
+        nc.sync.dma_start(place_list[:], offs4)
+        for t in range(PACK):
+            nc.sync.dma_start(out=users_raw[t][:], in_=users_by_place[:, t, :])
+        for b in range(E // P):
+            nc.sync.dma_start(out=vals_raw[b][:], in_=vals[b * P : (b + 1) * P, :])
+        for b in range(E // P):
+            nc.sync.dma_start(out=old_rows[b][:], in_=old[b * P : (b + 1) * P, :])
+
+        identity = tile("identity", [P, P], F32)
+        make_identity(nc, identity[:])
+        placed = [tile("placed%d" % b, [P, M], F32) for b in range(E // P)]
+        for b in range(E // P):
+            nc.gpsimd.memset(placed[b][:], 0.0)
+
+        picked_words = tile("picked_words", [P, I], U32)
+        picked_bytes = tile("picked_bytes", [P, I], U8)
+        keys = (picked_words, picked_bytes)
+        nc.vector.tensor_copy(
+            picked_bytes[:].rearrange("p (r s) -> p s r", r=PACK), key_bytes[:].indirect(token_list[:])
+        )
+
+        def quantise_notes(h, scalar_share):
+            grouped = tile("notes_grouped%d" % h, [P, BANK, PACK], BF16)
+            if scalar_share:
+                interleave(nc.scalar.copy, grouped[:, :scalar_share, :], notes_raw[h][:, :, :scalar_share])
+            interleave(nc.vector.tensor_copy, grouped[:, scalar_share:, :], notes_raw[h][:, :, scalar_share:])
+            return quantise("notes%d" % h, grouped, BANK)
+
+        wide = [tile("wide%d" % r, [P, U], F32) for r in range(PACK)]
+
+        def wide_half(h, notes_q, copy_out):
+            for r in range(PACK):
+                bank = ring_a.tile([P, BANK], F32, name="bank_a")
+                product(bank, keys, slice(r * P, (r + 1) * P), notes_q)
+                copy_out(wide[r][:, h * BANK : (h + 1) * BANK], bank[:])
+
+        notes_q0 = quantise_notes(0, 320)
+        nc.vector.tensor_copy(
+            picked_words[:].rearrange("p (r s) -> p s r", r=PACK), key_words[:].indirect(token_list[:])
+        )
+        wide_half(0, notes_q0, nc.scalar.copy)
+        notes_q1 = quantise_notes(1, 0)
+        wide_half(1, notes_q1, nc.vector.tensor_copy)
+
+        users_picked = tile("users_picked", [P, PACK, J], BF16)
+        for t in range(PACK - 1):
+            nc.scalar.activation(users_picked[:, t, :], users_raw[t][:].indirect(user_list[:]), COPY)
+        nc.vector.tensor_copy(users_picked[:, PACK - 1, :], users_raw[PACK - 1][:].indirect(user_list[:]))
+        looked_up = [tile(name, [P, J], F32) for name in ("users_raw3", "users_raw2", "users_raw1", "users_raw0")]
+        nc.vector.tensor_copy(looked_up[0][:], wide[0][:].indirect(note_list[:]))
+        users_grouped = tile("wide0", [P, J, PACK], BF16)
+        interleave(nc.vector.tensor_copy, users_grouped[:], users_picked[:])
+        users_q = quantise("users", users_grouped, J)
+        for r in range(1, PACK):
+            nc.scalar.activation(looked_up[r][:], wide[r][:].indirect(note_list[:]), COPY)
+
+        larger = [tile("larger%d" % r, [P, J], F32) for r in range(PACK)]
+        table = tile("table", [P, PACK, J], BF16)
+        for r in range(PACK):
+            bank = ring_b.tile([P, J], F32, name="bank_b")
+            product(bank, keys, slice(r * P, (r + 1) * P), users_q)
+            nc.vector.tensor_tensor(larger[r][:], looked_up[r][:], bank[:], ALU.max)
+        for r in range(PACK):
+            nc.vector.tensor_scalar(table[:, r, :], larger[r][:], factors[:, r : r + 1], None, ALU.mult)
+        table_grouped = tile("table_grouped", [P, J, PACK], BF16)
+        interleave(nc.vector.tensor_copy, table_grouped[:], table[:])
+        table_q = quantise("table", table_grouped, J)
+
+        values_grouped = []
+        picked = [tile("vals_picked%d" % b, [P, I], BF16) for b in range(E // P)]
+        for b in range(E // P):
+            nc.scalar.activation(picked[b][:], vals_raw[b][:].indirect(token_list[:]), COPY)
+        for b in range(E // P):
+            pairs = picked[b][:].bitcast(F32)
+            bank = ring_b.tile([P, 2, P], F32, name="bank_b")
+            for u in range(2):
+                nc.tensor.transpose(bank[:, u, :], pairs[:, u : I // 2 : 2], identity[:])
+            if b % 2 == 0:
+                values_grouped.append(tile("vals_raw%d" % (b + 1), [P, 2 * P, PACK], BF16))
+            first = P * (b % 2)
+            nc.scalar.copy(
+                values_grouped[-1][:, first : first + P, :].bitcast(F32), bank[:].rearrange("p u e -> p e u")
+            )
+
+        sums = [None] * (E // P)
+
+        def sum_block(b, copy_out, name):
+            bank = ring_a.tile([P, J], F32, name="bank_a")
+            first = P * (b % 2)
+            product(bank, values_q[b // 2], slice(first, first + P), table_q)
+            sums[b] = tile(name, [P, J], F32)
+            copy_out(sums[b][:], bank[:])
+
+        def place_on_vector(b, first, last):
+            nc.vector.tensor_copy(
+                placed[b][:].indirect(place_list[:, first // 16 : last // 16]), sums[b][:, first:last]
+            )
+
+        def place_on_scalar(b, first, last):
+            nc.scalar.activation(
+                placed[b][:].indirect(place_list[:, first // 16 : last // 16]), sums[b][:, first:last], COPY
+            )
+
+        def finish(b):
+            nc.vector.tensor_tensor(old_rows[b][:], old_rows[b][:], placed[b][:], ALU.add)
+            nc.sync.dma_start(out=out[b * P : (b + 1) * P, :], in_=old_rows[b][:])
+
+        values_q = [quantise("vals%d" % g, values_grouped[g], 2 * P, "larger%d" % (2 + g)) for g in range(2)]
+        sum_block(0, nc.vector.tensor_copy, "sums0")
+        sum_block(1, nc.scalar.copy, "vals_picked3")
+        place_on_vector(0, 0, J)
+        place_on_scalar(1, 0, J // 2)
+        place_on_scalar(1, J // 2, J)
+        finish(0)
+        sum_block(2, nc.scalar.copy, "sums2")
+        place_on_scalar(2, 0, J // 4)
+        sum_block(3, nc.scalar.copy, "sums3")
+        finish(1)
+        place_on_vector(2, J // 4, J)
+        place_on_scalar(3, 0, J // 2)
+        place_on_scalar(3, J // 2, J)
+        finish(2)
+        finish(3)

@@ -19,6 +19,7 @@ ALU = mybir.AluOpType
 P = 128
 PACK = 4
 BANK = 512
+SCALAR_PART = 160
 
 
 def tile_attend_tab_wideandown_put_kernel(
@@ -135,29 +136,33 @@ def tile_attend_tab_wideandown_put_kernel(
         notes_q1 = quantise_notes(1, 0)
         wide_half(1, notes_q1, nc.vector.tensor_copy)
 
-        users_picked = tile("users_picked", [P, PACK, J], BF16)
-        for t in range(PACK - 1):
+        users_picked = tile("notes_grouped1", [P, PACK, J], BF16)
+        nc.vector.tensor_copy(users_picked[:, 0, :], users_raw[0][:].indirect(user_list[:]))
+        for t in range(1, PACK):
             nc.scalar.activation(users_picked[:, t, :], users_raw[t][:].indirect(user_list[:]), COPY)
-        nc.vector.tensor_copy(users_picked[:, PACK - 1, :], users_raw[PACK - 1][:].indirect(user_list[:]))
-        looked_up = [tile(name, [P, J], F32) for name in ("users_raw3", "users_raw2", "users_raw1", "users_raw0")]
-        nc.vector.tensor_copy(looked_up[0][:], wide[0][:].indirect(note_list[:]))
+        looked_up = [None] * PACK
+        looked_up[0] = tile("looked_up0", [P, J], F32)[:]
+        nc.vector.tensor_copy(looked_up[0], wide[0][:].indirect(note_list[:]))
         users_grouped = tile("wide0", [P, J, PACK], BF16)
         interleave(nc.vector.tensor_copy, users_grouped[:], users_picked[:])
         users_q = quantise("users", users_grouped, J)
-        for r in range(1, PACK):
-            nc.scalar.activation(looked_up[r][:], wide[r][:].indirect(note_list[:]), COPY)
+        looked_up[1] = tile("wide0", [P, J], F32)[:]
+        nc.vector.tensor_copy(looked_up[1], wide[1][:].indirect(note_list[:]))
+        looked_up_last = tile("users_raw3", [P, 2, J], F32)
+        for r in range(2, PACK):
+            looked_up[r] = looked_up_last[:, r - 2, :]
+            nc.scalar.activation(looked_up[r], wide[r][:].indirect(note_list[:]), COPY)
 
         larger = [tile("larger%d" % r, [P, J], F32) for r in range(PACK)]
         table = tile("table", [P, PACK, J], BF16)
         for r in range(PACK):
             bank = ring_b.tile([P, J], F32, name="bank_b")
             product(bank, keys, slice(r * P, (r + 1) * P), users_q)
-            nc.vector.tensor_tensor(larger[r][:], looked_up[r][:], bank[:], ALU.max)
+            nc.vector.tensor_tensor(larger[r][:], looked_up[r], bank[:], ALU.max)
         for r in range(PACK):
             nc.vector.tensor_scalar(table[:, r, :], larger[r][:], factors[:, r : r + 1], None, ALU.mult)
         table_grouped = tile("table_grouped", [P, J, PACK], BF16)
         interleave(nc.vector.tensor_copy, table_grouped[:], table[:])
-        table_q = quantise("table", table_grouped, J)
 
         values_grouped = []
         picked = [tile("vals_picked%d" % b, [P, I], BF16) for b in range(E // P)]
@@ -169,48 +174,53 @@ def tile_attend_tab_wideandown_put_kernel(
             for u in range(2):
                 nc.tensor.transpose(bank[:, u, :], pairs[:, u : I // 2 : 2], identity[:])
             if b % 2 == 0:
-                values_grouped.append(tile("vals_raw%d" % (b + 1), [P, 2 * P, PACK], BF16))
+                values_grouped.append(tile("vals_raw2" if b == 0 else "vals_grouped1", [P, 2 * P, PACK], BF16))
             first = P * (b % 2)
             nc.scalar.copy(
                 values_grouped[-1][:, first : first + P, :].bitcast(F32), bank[:].rearrange("p u e -> p e u")
             )
 
-        sums = [None] * (E // P)
+        values_q = [quantise("vals0", values_grouped[0], 2 * P, "table")]
+        table_q = quantise("table", table_grouped, J)
+        banks = []
 
-        def sum_block(b, copy_out, name):
-            bank = ring_a.tile([P, J], F32, name="bank_a")
-            first = P * (b % 2)
-            product(bank, values_q[b // 2], slice(first, first + P), table_q)
-            sums[b] = tile(name, [P, J], F32)
-            copy_out(sums[b][:], bank[:])
+        def multiply_pair(g):
+            for half in range(2):
+                banks.append(ring_a.tile([P, J], F32, name="bank_a"))
+                product(banks[-1], values_q[g], slice(half * P, (half + 1) * P), table_q)
 
-        def place_on_vector(b, first, last):
-            nc.vector.tensor_copy(
-                placed[b][:].indirect(place_list[:, first // 16 : last // 16]), sums[b][:, first:last]
-            )
+        def copy_out(copy, b, first, last, name):
+            sums = tile(name, [P, last - first], F32)
+            copy(sums[:], banks[b][:, first:last])
+            return sums
 
-        def place_on_scalar(b, first, last):
-            nc.scalar.activation(
-                placed[b][:].indirect(place_list[:, first // 16 : last // 16]), sums[b][:, first:last], COPY
-            )
+        def window(b, first, last):
+            return placed[b][:].indirect(place_list[:, first // 16 : last // 16])
 
-        def finish(b):
-            nc.vector.tensor_tensor(old_rows[b][:], old_rows[b][:], placed[b][:], ALU.add)
-            nc.sync.dma_start(out=out[b * P : (b + 1) * P, :], in_=old_rows[b][:])
+        def finish(b, result, pieces=1):
+            width = M // pieces
+            for first in range(0, M, width):
+                columns = slice(first, first + width)
+                nc.vector.tensor_tensor(result[:, columns], old_rows[b][:, columns], placed[b][:, columns], ALU.add)
+                nc.sync.dma_start(out=out[b * P : (b + 1) * P, columns], in_=result[:, columns])
 
-        values_q = [quantise("vals%d" % g, values_grouped[g], 2 * P, "larger%d" % (2 + g)) for g in range(2)]
-        sum_block(0, nc.vector.tensor_copy, "sums0")
-        sum_block(1, nc.scalar.copy, "vals_picked3")
-        place_on_vector(0, 0, J)
-        place_on_scalar(1, 0, J // 2)
-        place_on_scalar(1, J // 2, J)
-        finish(0)
-        sum_block(2, nc.scalar.copy, "sums2")
-        place_on_scalar(2, 0, J // 4)
-        sum_block(3, nc.scalar.copy, "sums3")
-        finish(1)
-        place_on_vector(2, J // 4, J)
-        place_on_scalar(3, 0, J // 2)
-        place_on_scalar(3, J // 2, J)
-        finish(2)
-        finish(3)
+        def whole_on_scalar(b, name):
+            sums = copy_out(nc.scalar.copy, b, 0, J, name)
+            for first in (0, J // 2):
+                nc.scalar.activation(window(b, first, first + J // 2), sums[:, first : first + J // 2], COPY)
+
+        multiply_pair(0)
+        sums0 = copy_out(nc.vector.tensor_copy, 0, 0, J, "sums0")
+        nc.vector.tensor_copy(window(0, 0, J), sums0[:])
+        whole_on_scalar(1, "vals_raw3")
+        values_q.append(quantise("vals1", values_grouped[1], 2 * P, "sums0"))
+        multiply_pair(1)
+        finish(0, tile("vals_grouped1", [P, M], F32))
+        head = copy_out(nc.scalar.copy, 2, 0, SCALAR_PART, "late_sums")
+        nc.scalar.activation(window(2, 0, SCALAR_PART), head[:], COPY)
+        finish(1, old_rows[1])
+        rest = copy_out(nc.vector.tensor_copy, 2, SCALAR_PART, J, "placed1")
+        nc.vector.tensor_copy(window(2, SCALAR_PART, J), rest[:])
+        whole_on_scalar(3, "late_sums")
+        finish(2, old_rows[2], 2)
+        finish(3, tile("placed1", [P, M], F32), 2)

@@ -19,7 +19,6 @@ ALU = mybir.AluOpType
 P = 128
 PACK = 4
 BANK = 512
-SCALAR_PART = 160
 
 
 def tile_attend_tab_wideandown_put_kernel(
@@ -104,7 +103,7 @@ def tile_attend_tab_wideandown_put_kernel(
         make_identity(nc, identity[:])
         placed = [tile("placed%d" % b, [P, M], F32) for b in range(E // P)]
         for b in range(E // P):
-            nc.gpsimd.memset(placed[b][:], 0.0)
+            (nc.vector if b % 2 == 0 else nc.gpsimd).memset(placed[b][:], 0.0)
 
         picked_words = tile("picked_words", [P, I], U32)
         picked_bytes = tile("picked_bytes", [P, I], U8)
@@ -197,11 +196,11 @@ def tile_attend_tab_wideandown_put_kernel(
         def window(b, first, last):
             return placed[b][:].indirect(place_list[:, first // 16 : last // 16])
 
-        def finish(b, result, pieces=1):
+        def finish(engine, b, result, pieces=1):
             width = M // pieces
             for first in range(0, M, width):
                 columns = slice(first, first + width)
-                nc.vector.tensor_tensor(result[:, columns], old_rows[b][:, columns], placed[b][:, columns], ALU.add)
+                engine.tensor_tensor(result[:, columns], old_rows[b][:, columns], placed[b][:, columns], ALU.add)
                 nc.sync.dma_start(out=out[b * P : (b + 1) * P, columns], in_=result[:, columns])
 
         def whole_on_scalar(b, name):
@@ -210,17 +209,17 @@ def tile_attend_tab_wideandown_put_kernel(
                 nc.scalar.activation(window(b, first, first + J // 2), sums[:, first : first + J // 2], COPY)
 
         multiply_pair(0)
-        sums0 = copy_out(nc.vector.tensor_copy, 0, 0, J, "sums0")
-        nc.vector.tensor_copy(window(0, 0, J), sums0[:])
+        first_half = copy_out(nc.vector.tensor_copy, 0, 0, J // 2, "sums0")
+        nc.vector.tensor_copy(window(0, 0, J // 2), first_half[:])
         whole_on_scalar(1, "vals_raw3")
-        values_q.append(quantise("vals1", values_grouped[1], 2 * P, "sums0"))
+        values_q.append(quantise("vals1", values_grouped[1], 2 * P))
         multiply_pair(1)
-        finish(0, tile("vals_grouped1", [P, M], F32))
-        head = copy_out(nc.scalar.copy, 2, 0, SCALAR_PART, "late_sums")
-        nc.scalar.activation(window(2, 0, SCALAR_PART), head[:], COPY)
-        finish(1, old_rows[1])
-        rest = copy_out(nc.vector.tensor_copy, 2, SCALAR_PART, J, "placed1")
-        nc.vector.tensor_copy(window(2, SCALAR_PART, J), rest[:])
-        whole_on_scalar(3, "late_sums")
-        finish(2, old_rows[2], 2)
-        finish(3, tile("placed1", [P, M], F32), 2)
+        second_half = copy_out(nc.vector.tensor_copy, 0, J // 2, J, "vals_grouped1")
+        nc.vector.tensor_copy(window(0, J // 2, J), second_half[:])
+        finish(nc.gpsimd, 0, old_rows[0])
+        finish(nc.gpsimd, 1, old_rows[1])
+        sums2 = copy_out(nc.vector.tensor_copy, 2, 0, J, "vals_grouped1")
+        nc.vector.tensor_copy(window(2, 0, J), sums2[:])
+        whole_on_scalar(3, "vals_raw3")
+        finish(nc.vector, 2, tile("placed1", [P, M], F32), 2)
+        finish(nc.vector, 3, tile("vals_grouped1", [P, M], F32), 2)

from contextlib import ExitStack

import concourse.mybir as mybir
from concourse.masks import make_identity

D, T, I, J, U, Z, E, M = 512, 2048, 512, 512, 1024, 1024, 512, 1024
FLOPS = 2 * D * I * U + 2 * D * I * J + 2 * I * E * J

F32 = mybir.dt.float32
BF16 = mybir.dt.bfloat16
I32 = mybir.dt.int32
U32 = mybir.dt.uint32
U16 = mybir.dt.uint16
U8 = mybir.dt.uint8
FP8X4 = mybir.dt.float8_e4m3fn_x4
COPY = mybir.ActivationFunctionType.Copy
ALU = mybir.AluOpType

P = 128
PACK = 4
BANK = 512


def tile_attend_tab_wideandown_put_kernel(
    tc, keys_words, keys_scales, notes, users2, rowf, vals, old, offs, offs2, offs3, offs4, out
):
    nc = tc.nc
    with ExitStack() as ctx:
        sb = ctx.enter_context(tc.tile_pool(name="sb", bufs=1))
        ring_a = ctx.enter_context(tc.psum_pool(name="ring_a", bufs=4))
        ring_b = ctx.enter_context(tc.psum_pool(name="ring_b", bufs=4))

        def tile(name, shape, dtype):
            return sb.tile(shape, dtype, name=name, align_bytes=64)

        def quantise(name, grouped, width, codes_name=None):
            codes = tile(codes_name or name + "_codes", [P, width], U32)
            scales = tile(name + "_scales", [P, width], U8)
            nc.vector.quantize_mx(
                out=codes[:].bitcast(FP8X4),
                scales=scales[:],
                in_=grouped[:].rearrange("p w t -> p (w t)"),
            )
            return codes, scales

        def interleave(copy, grouped, planes):
            copy(
                grouped.rearrange("p (c i) t -> p c t i", i=4),
                planes.rearrange("p t (c i) -> p c t i", i=4),
            )

        def product(bank, stationary, columns, moving):
            nc.tensor.matmul_mx(
                out=bank[:],
                lhsT=stationary[0][:, columns].bitcast(FP8X4),
                lhsT_scale=stationary[1][:, columns],
                rhs=moving[0][:].bitcast(FP8X4),
                rhs_scale=moving[1][:],
                start=True,
                stop=True,
            )

        token_list = tile("token_list", [P, I // 16], U16)
        note_list = tile("note_list", [P, J // 16], U16)
        user_list = tile("user_list", [P, J // 16], U16)
        place_list = tile("place_list", [P, J // 16], U16)
        key_words = tile("key_words", [P, T], U32)
        key_bytes = tile("key_bytes", [P, T], U8)
        notes_raw = [tile("notes_raw%d" % h, [P, PACK, BANK], F32) for h in range(U // BANK)]
        users_raw = [tile("users_raw%d" % t, [P, Z], F32) for t in range(PACK)]
        vals_raw = [tile("vals_raw%d" % b, [P, T], F32) for b in range(E // P)]
        old_rows = [tile("old_rows%d" % b, [P, M], F32) for b in range(E // P)]
        factors = tile("factors", [P, PACK], F32)

        nc.gpsimd.memset(key_bytes[:].bitcast(I32), 0)
        notes_by_place = notes.rearrange("(p t) u -> p t u", t=PACK)
        users_by_place = users2.rearrange("(p t) z -> p t z", t=PACK)

        nc.sync.dma_start(token_list[:], offs)
        nc.sync.dma_start(user_list[:], offs3)
        nc.sync.dma_start(note_list[:], offs2)
        nc.sync.dma_start(out=factors[:], in_=rowf.rearrange("(p r) one -> p (r one)", r=PACK))
        nc.sync.dma_start(out=notes_raw[0][:], in_=notes_by_place[:, :, 0:BANK])
        for q in range(4):
            nc.scalar.dma_start(
                out=key_bytes[32 * q : 32 * q + 4, :].bitcast(I32),
                in_=keys_scales[0, 4 * q : 4 * q + 4, :].bitcast(I32),
            )
        nc.sync.dma_start(
            out=key_words[:].bitcast(I32),
            in_=keys_words[0].rearrange("p n t -> p (n t)").bitcast(I32),
        )
        nc.sync.dma_start(out=notes_raw[1][:], in_=notes_by_place[:, :, BANK:U])
        nc.sync.dma_start(place_list[:], offs4)
        for t in range(PACK):
            nc.sync.dma_start(out=users_raw[t][:], in_=users_by_place[:, t, :])
        for b in range(E // P):
            nc.sync.dma_start(out=vals_raw[b][:], in_=vals[b * P : (b + 1) * P, :])
        for b in range(E // P):
            nc.sync.dma_start(out=old_rows[b][:], in_=old[b * P : (b + 1) * P, :])

        identity = tile("identity", [P, P], F32)
        make_identity(nc, identity[:])
        placed = [tile("placed%d" % b, [P, M], F32) for b in range(E // P)]
        for b in range(E // P):
            (nc.vector if b % 2 == 0 else nc.gpsimd).memset(placed[b][:], 0.0)

        picked_words = tile("picked_words", [P, I], U32)
        picked_bytes = tile("picked_bytes", [P, I], U8)
        keys = (picked_words, picked_bytes)
        nc.vector.tensor_copy(
            picked_bytes[:].rearrange("p (r s) -> p s r", r=PACK), key_bytes[:].indirect(token_list[:])
        )

        def quantise_notes(h, scalar_share):
            grouped = tile("notes_grouped%d" % h, [P, BANK, PACK], BF16)
            if scalar_share:
                interleave(nc.scalar.copy, grouped[:, :scalar_share, :], notes_raw[h][:, :, :scalar_share])
            interleave(nc.vector.tensor_copy, grouped[:, scalar_share:, :], notes_raw[h][:, :, scalar_share:])
            return quantise("notes%d" % h, grouped, BANK)

        wide = [tile("wide%d" % r, [P, U], F32) for r in range(PACK)]

        def wide_half(h, notes_q, copy_out):
            for r in range(PACK):
                bank = ring_a.tile([P, BANK], F32, name="bank_a")
                product(bank, keys, slice(r * P, (r + 1) * P), notes_q)
                copy_out(wide[r][:, h * BANK : (h + 1) * BANK], bank[:])

        notes_q0 = quantise_notes(0, 320)
        nc.vector.tensor_copy(
            picked_words[:].rearrange("p (r s) -> p s r", r=PACK), key_words[:].indirect(token_list[:])
        )
        wide_half(0, notes_q0, nc.scalar.copy)
        notes_q1 = quantise_notes(1, 0)
        wide_half(1, notes_q1, nc.vector.tensor_copy)

        users_picked = tile("notes_grouped1", [P, PACK, J], BF16)
        nc.vector.tensor_copy(users_picked[:, 0, :], users_raw[0][:].indirect(user_list[:]))
        for t in range(1, PACK):
            nc.scalar.activation(users_picked[:, t, :], users_raw[t][:].indirect(user_list[:]), COPY)
        looked_up = [None] * PACK
        looked_up[0] = tile("looked_up0", [P, J], F32)[:]
        nc.vector.tensor_copy(looked_up[0], wide[0][:].indirect(note_list[:]))
        users_grouped = tile("wide0", [P, J, PACK], BF16)
        interleave(nc.vector.tensor_copy, users_grouped[:], users_picked[:])
        users_q = quantise("users", users_grouped, J)
        looked_up[1] = tile("wide0", [P, J], F32)[:]
        nc.vector.tensor_copy(looked_up[1], wide[1][:].indirect(note_list[:]))
        looked_up_last = tile("users_raw3", [P, 2, J], F32)
        for r in range(2, PACK):
            looked_up[r] = looked_up_last[:, r - 2, :]
            nc.scalar.activation(looked_up[r], wide[r][:].indirect(note_list[:]), COPY)

        larger = [tile("larger%d" % r, [P, J], F32) for r in range(PACK)]
        table = tile("table", [P, PACK, J], BF16)
        for r in range(PACK):
            bank = ring_b.tile([P, J], F32, name="bank_b")
            product(bank, keys, slice(r * P, (r + 1) * P), users_q)
            nc.vector.tensor_tensor(larger[r][:], looked_up[r], bank[:], ALU.max)
        for r in range(PACK):
            nc.vector.tensor_scalar(table[:, r, :], larger[r][:], factors[:, r : r + 1], None, ALU.mult)
        table_grouped = tile("table_grouped", [P, J, PACK], BF16)
        interleave(nc.vector.tensor_copy, table_grouped[:], table[:])

        values_grouped = []
        picked = [tile("vals_picked%d" % b, [P, I], BF16) for b in range(E // P)]
        for b in range(E // P):
            nc.scalar.activation(picked[b][:], vals_raw[b][:].indirect(token_list[:]), COPY)
        for b in range(E // P):
            pairs = picked[b][:].bitcast(F32)
            bank = ring_b.tile([P, 2, P], F32, name="bank_b")
            for u in range(2):
                nc.tensor.transpose(bank[:, u, :], pairs[:, u : I // 2 : 2], identity[:])
            if b % 2 == 0:
                values_grouped.append(tile("vals_raw2" if b == 0 else "vals_grouped1", [P, 2 * P, PACK], BF16))
            first = P * (b % 2)
            nc.scalar.copy(
                values_grouped[-1][:, first : first + P, :].bitcast(F32), bank[:].rearrange("p u e -> p e u")
            )

        values_q = [quantise("vals0", values_grouped[0], 2 * P, "table")]
        table_q = quantise("table", table_grouped, J)
        banks = []

        def multiply_pair(g):
            for half in range(2):
                banks.append(ring_a.tile([P, J], F32, name="bank_a"))
                product(banks[-1], values_q[g], slice(half * P, (half + 1) * P), table_q)

        def copy_out(copy, b, first, last, name):
            sums = tile(name, [P, last - first], F32)
            copy(sums[:], banks[b][:, first:last])
            return sums

        def window(b, first, last):
            return placed[b][:].indirect(place_list[:, first // 16 : last // 16])

        def finish(engine, b, result, pieces=1):
            width = M // pieces
            for first in range(0, M, width):
                columns = slice(first, first + width)
                engine.tensor_tensor(result[:, columns], old_rows[b][:, columns], placed[b][:, columns], ALU.add)
                nc.sync.dma_start(out=out[b * P : (b + 1) * P, columns], in_=result[:, columns])

        def whole_on_scalar(b, name):
            sums = copy_out(nc.scalar.copy, b, 0, J, name)
            for first in (0, J // 2):
                nc.scalar.activation(window(b, first, first + J // 2), sums[:, first : first + J // 2], COPY)

        multiply_pair(0)
        first_half = copy_out(nc.vector.tensor_copy, 0, 0, J // 2, "sums0")
        nc.vector.tensor_copy(window(0, 0, J // 2), first_half[:])
        whole_on_scalar(1, "vals_raw3")
        values_q.append(quantise("vals1", values_grouped[1], 2 * P))
        multiply_pair(1)
        second_half = copy_out(nc.vector.tensor_copy, 0, J // 2, J, "vals_grouped1")
        nc.vector.tensor_copy(window(0, J // 2, J), second_half[:])
        finish(nc.gpsimd, 0, old_rows[0])
        finish(nc.gpsimd, 1, old_rows[1])
        sums2 = copy_out(nc.vector.tensor_copy, 2, 0, J, "vals_grouped1")
        nc.vector.tensor_copy(window(2, 0, J), sums2[:])
        whole_on_scalar(3, "vals_raw3")
        finish(nc.vector, 2, tile("placed1", [P, M], F32), 2)
        finish(nc.vector, 3, tile("vals_grouped1", [P, M], F32), 2)
